import numpy as np
import ml_dtypes


def mxq(x, axis, fmt="e4m3"):
    dtype, down = {"e4m3": (ml_dtypes.float8_e4m3fn, 7), "e5m2": (ml_dtypes.float8_e5m2, 14)}[fmt]
    v = np.moveaxis(np.asarray(x, np.float32).astype(ml_dtypes.bfloat16).astype(np.float64), axis, -1)
    blocks = v.reshape(v.shape[:-1] + (-1, 32))
    amax = np.abs(blocks).max(-1, keepdims=True)
    byte = np.maximum(np.where(amax > 0, np.frexp(amax)[1] - 1 + 127, 0) - down, 1)
    scale = np.exp2(byte - 127.0)
    codes = (blocks / scale).astype(np.float32).astype(dtype).astype(np.float64)
    return np.moveaxis((codes * scale).reshape(v.shape), -1, axis)


WIDE = False


def mx_kscale(k):
    if not WIDE:
        return np.ones(k)
    levels = np.array([10, -10, 5, -5, 0])
    if k % 512:
        return np.exp2(np.random.permutation(np.resize(levels, k // 32))).repeat(32)
    a = np.empty((k // 512, 16))
    for p in range(k // 512):
        a[p, :8] = np.random.permutation(np.resize(levels, 8))
        for g in range(8):
            far = levels[np.abs(levels - a[p, g]) >= 10]
            a[p, g + 8] = far[np.random.randint(len(far))]
    return np.exp2(a.ravel()).repeat(32)


def f64(x):
    return np.asarray(x).astype(np.float64)


def striped(idx):
    return np.tile(idx.reshape(-1, 16).T, (8, 1)).astype(np.uint16)


def unstriped(offs):
    return offs[:16].T.reshape(-1).astype(np.int64)


def relu(v):
    return np.maximum(v, 0.0)


K, T, E, C, N = 512, 512, 6, 256, 512
TOP = 3
M = 512


def by_expert(wq, xq):
    return np.concatenate([wq[e].T @ xq[:, e * C:(e + 1) * C] for e in range(E)], axis=1)


def setup_inputs():
    n = np.random.standard_normal
    s = mx_kscale(K)[:, None]
    v = mx_kscale(N)
    deal = np.repeat(np.arange(E), C).reshape(TOP, T)[:, np.random.permutation(T)]
    deal = np.take_along_axis(deal, np.argsort(np.random.rand(TOP, T), axis=0), axis=0)
    for _ in range(8):
        s_, t_ = np.random.permutation(T).reshape(2, -1); r = np.random.randint(TOP, size=T // 2); x, y = deal[r, s_].copy(), deal[r, t_].copy()
        ok = ~((deal[:, s_] == y).any(0) | (deal[:, t_] == x).any(0)); deal[r[ok], s_[ok]] = y[ok]; deal[r[ok], t_[ok]] = x[ok]
    order = np.lexsort((np.random.rand(TOP * T), deal.reshape(-1)))
    slot_token = order % T; pos = np.empty(TOP * T, np.int64); pos[order] = np.arange(TOP * T); pos = pos.reshape(TOP, T)
    g = np.random.uniform(0.5, 1.5, (TOP, T)); g = g / g.sum(0)
    return {
        "xT": (n((K, T)) * s).astype(np.float32),
        "w": (n((E, K, N)) / np.sqrt(K) / s[None] * v[None, None, :]).astype(np.float32),
        "b": (0.3 * n((N, E)) * v[:, None]).astype(np.float32),
        "wp": (n((N, M)) / np.sqrt(N) / v[:, None]).astype(np.float32),
        "gate": np.stack([np.tile(r, (N, 1)) for r in g]).astype(np.float32),
        "offs": striped(slot_token),
        "pos1": striped(pos[0]),
        "pos2": striped(pos[1]),
        "pos3": striped(pos[2]),
    }


def reference(xT, w, b, wp, gate, offs, pos1, pos2, pos3):
    idx = unstriped(offs)
    xq = mxq(f64(xT)[:, idx], 0, "e4m3")
    y = by_expert(mxq(f64(w), 1, "e4m3"), xq)
    y = relu(y + np.repeat(f64(b), C, axis=1))
    c = f64(gate[0]) * y[:, unstriped(pos1)] + f64(gate[1]) * y[:, unstriped(pos2)] + f64(gate[2]) * y[:, unstriped(pos3)]
    return mxq(f64(wp), 0, "e4m3").T @ mxq(c, 0, "e4m3")

@@ -1,0 +1,232 @@
+from contextlib import ExitStack
+
+import concourse.mybir as mybir
+from concourse.masks import make_identity
+
+K, T, E, C, N, M = 512, 512, 6, 256, 512, 512
+TOP = 3
+S = E * C
+FLOPS = 2 * K * N * S + 2 * N * M * T
+
+F32 = mybir.dt.float32
+BF16 = mybir.dt.bfloat16
+I32 = mybir.dt.int32
+U32 = mybir.dt.uint32
+U16 = mybir.dt.uint16
+U8 = mybir.dt.uint8
+FP8X4 = mybir.dt.float8_e4m3fn_x4
+RELU = mybir.ActivationFunctionType.Relu
+COPY = mybir.ActivationFunctionType.Copy
+MULT = mybir.AluOpType.mult
+
+P = 128
+PACK = 4
+HALF = 256
+LIST_ROWS = 16
+TOKEN_GROUPS = ((0, 256), (256, 128), (384, 128))
+KIB = 1024
+PLACES = {
+    "w_grouped00": 0, "slot_words1": 0, "slot_scales1": 2 * KIB,
+    "w_grouped01": 4 * KIB, "slot_words2": 4 * KIB, "slot_scales2": 6 * KIB,
+    "w_grouped02": 8 * KIB, "w_grouped10": 8 * KIB,
+    "y0": 12 * KIB + 64, "w_raw03": 18 * KIB, "y1": 22 * KIB - 64,
+    "bias0": 28 * KIB, "w_grouped11": 28 * KIB,
+    "w_raw13": 32 * KIB, "w_grouped12": 32 * KIB, "products1_0": 32 * KIB,
+    "y2": 38 * KIB + 64, "w_raw15": 44 * KIB, "y3": 48 * KIB - 64,
+    "bias1": 54 * KIB, "wp_grouped": 54 * KIB,
+    "c_rows0": 58 * KIB, "products2_384": 58 * KIB,
+    "c_rows1": 60 * KIB, "products3_384": 60 * KIB,
+}
+VECTOR_COPIES = ((1, 0), (1, 1))
+
+
+def tile_moe_nxt_lin_relu_kernel(tc, xT, w, b, wp, gate, offs, pos1, pos2, pos3, out):
+    nc = tc.nc
+    with ExitStack() as ctx:
+        lists = ctx.enter_context(tc.tile_pool(name="lists", bufs=1))
+        keep = ctx.enter_context(tc.tile_pool(name="keep", bufs=1))
+        shared = ctx.enter_context(tc.tile_pool(name="shared", bufs=1))
+        work_psum = ctx.enter_context(tc.psum_pool(name="work_psum", bufs=4))
+        sum_psum = ctx.enter_context(tc.psum_pool(name="sum_psum", bufs=1))
+
+        def sbuf(name, shape, dtype):
+            if name in PLACES:
+                return shared.tile(shape, dtype, name=name, align_bytes=64, offset=PLACES[name])
+            return keep.tile(shape, dtype, name=name, align_bytes=64)
+
+        def load_rows(name, rows):
+            raw = sbuf(name, [P, PACK, HALF], F32)
+            nc.sync.dma_start(out=raw[:], in_=rows.rearrange("(p j) c -> p j c", j=PACK))
+            return raw
+
+        def load_list(name, src):
+            tile = lists.tile(list(src.shape), U16, name=name)
+            nc.sync.dma_start(tile[:], src)
+            return tile
+
+        def interleave(raw, on_vector, grouped):
+            dst = grouped.rearrange("p (c i) j -> p c j i", i=2)
+            src = raw[:].rearrange("p j (c i) -> p c j i", i=2)
+            if on_vector:
+                nc.vector.tensor_copy(out=dst, in_=src)
+            else:
+                nc.scalar.activation(out=dst, in_=src, func=COPY)
+
+        def quantize(grouped, codes, scales):
+            nc.vector.quantize_mx(out=codes.bitcast(FP8X4), scales=scales,
+                                  in_=grouped[:].rearrange("p c j -> p (c j)"))
+
+        halves = [slice(h * HALF, (h + 1) * HALF) for h in range(2)]
+
+        x_raw = [load_rows("x_raw%d" % h, xT[:, halves[h]]) for h in range(2)]
+        slot_tokens = load_list("slot_tokens", offs)
+        w_raw = {}
+        w_raw[0, 0] = load_rows("w_raw00", w[0][:, halves[0]])
+        w_raw[0, 1] = load_rows("w_raw01", w[1][:, halves[0]])
+        bias = [sbuf("bias%d" % h, [P, 2, E], F32) for h in range(2)]
+        for h in range(2):
+            nc.sync.dma_start(out=bias[h][:], in_=b[halves[h], :].rearrange("(s p) e -> p s e", p=P))
+        for e in range(2, E):
+            w_raw[0, e] = load_rows("w_raw0%d" % e, w[e][:, halves[0]])
+        for e in range(2):
+            w_raw[1, e] = load_rows("w_raw1%d" % e, w[e][:, halves[1]])
+        token_slots = [load_list("token_slots%d" % i, src) for i, src in enumerate((pos1, pos2, pos3))]
+        gates = sbuf("gates", [P, TOP, T], F32)
+        nc.sync.dma_start(out=gates[:], in_=gate[:, 0:P, :].rearrange("i p t -> p i t"))
+        for e in range(2, E):
+            w_raw[1, e] = load_rows("w_raw1%d" % e, w[e][:, halves[1]])
+        wp_raw = [load_rows("wp_raw%d" % h, wp[:, halves[h]]) for h in range(2)]
+
+        identity = sbuf("identity", [P, P], F32)
+        make_identity(nc, identity[:])
+
+        x_words = sbuf("x_words", [P, 2 * T], U32)
+        x_scales = sbuf("x_scales", [P, 2 * T], U8)
+        nc.gpsimd.memset(x_words[:, T:], 0)
+        nc.gpsimd.memset(x_scales[:].bitcast(I32), 0)
+        for h in range(2):
+            x_grouped = sbuf("x_grouped%d" % h, [P, HALF, PACK], BF16)
+            interleave(x_raw[h], True, x_grouped[:])
+            quantize(x_grouped, x_words[:, halves[h]], x_scales[:, halves[h]])
+
+        y = [sbuf("y%d" % r, [P, S], F32) for r in range(N // P)]
+        slot_words, slot_scales = {}, {}
+        w_words, w_scales = {}, {}
+
+        def gather_tokens(pair):
+            cols = slice(pair * 2 * C // LIST_ROWS, (pair + 1) * 2 * C // LIST_ROWS)
+            slot_words[pair] = sbuf("slot_words%d" % pair, [P, 2 * C], U32)
+            slot_scales[pair] = sbuf("slot_scales%d" % pair, [P, 2 * C], U8)
+            nc.vector.tensor_copy(slot_words[pair][:], x_words[:].indirect(slot_tokens[:, cols]))
+            nc.vector.tensor_copy(slot_scales[pair][:], x_scales[:].indirect(slot_tokens[:, cols]))
+
+        def quantize_weights(h, pair):
+            grouped = sbuf("w_grouped%d%d" % (h, pair), [P, 2 * HALF, PACK], BF16)
+            for n in range(2):
+                e = 2 * pair + n
+                interleave(w_raw[h, e], (h, e) in VECTOR_COPIES, grouped[:, halves[n], :])
+            w_words[h, pair] = sbuf("w_words%d%d" % (h, pair), [P, 2 * HALF], U32)
+            w_scales[h, pair] = sbuf("w_scales%d%d" % (h, pair), [P, 2 * HALF], U8)
+            quantize(grouped, w_words[h, pair][:], w_scales[h, pair][:])
+
+        def expert(h, e):
+            acc = work_psum.tile([P, 2, C], F32, name="acc")
+            mine = slice((e % 2) * C, (e % 2 + 1) * C)
+            for s in range(2):
+                cols = slice((e % 2) * HALF + s * P, (e % 2) * HALF + (s + 1) * P)
+                nc.tensor.matmul_mx(out=acc[:, s, :],
+                                    lhsT=w_words[h, e // 2][:, cols].bitcast(FP8X4), lhsT_scale=w_scales[h, e // 2][:, cols],
+                                    rhs=slot_words[e // 2][:, mine].bitcast(FP8X4), rhs_scale=slot_scales[e // 2][:, mine],
+                                    start=True, stop=True)
+            return acc
+
+        def expert_pair(h, pair):
+            accs = [(e, expert(h, e)) for e in (2 * pair, 2 * pair + 1)]
+            for s in range(2):
+                r = 2 * h + s
+                for e, acc in accs:
+                    nc.scalar.activation(out=y[r][:, e * C:(e + 1) * C], in_=acc[:, s, :], func=RELU,
+                                         bias=bias[h][:, s, e:e + 1])
+
+        c_sum = [sum_psum.tile([P, N], F32, name="c_sum%d" % q) for q in range(T // P)]
+        c_rows = [sbuf("c_rows%d" % q, [P, 2, P, 2], BF16) for q in range(T // P)]
+
+        def combine(r, t0, width):
+            products = sbuf("products%d_%d" % (r, t0), [P, TOP, width], F32)
+            for i in range(TOP):
+                product = products[:, i, :]
+                offsets = token_slots[i][:, t0 // LIST_ROWS:(t0 + width) // LIST_ROWS]
+                nc.vector.tensor_tensor(product, y[r][:].indirect(offsets), gates[:, i, t0:t0 + width], MULT)
+                for s in range(width // P):
+                    nc.tensor.matmul(c_sum[t0 // P + s][:, r * P:(r + 1) * P], lhsT=product[:, s * P:(s + 1) * P],
+                                     rhs=identity[:], is_transpose=True, start=(i == 0), stop=(i == TOP - 1))
+
+        def round_sums(q, h):
+            nc.scalar.copy(out=c_rows[q][:, :, h * 64:(h + 1) * 64, :],
+                           in_=c_sum[q][:, halves[h]].rearrange("t (p u e) -> t u p e", u=2, e=2))
+
+        gather_tokens(0)
+        for pair in range(E // 2):
+            quantize_weights(0, pair)
+            if pair + 1 < E // 2:
+                gather_tokens(pair + 1)
+            if pair > 0:
+                expert_pair(0, pair - 1)
+        expert_pair(0, E // 2 - 1)
+
+        quantize_weights(1, 0)
+        combine(0, 0, T)
+        quantize_weights(1, 1)
+        quantize_weights(1, 2)
+        for pair in range(E // 2):
+            expert_pair(1, pair)
+        combine(1, 0, T)
+
+        wp_words = sbuf("wp_words", [P, M], U32)
+        wp_scales = sbuf("wp_scales", [P, M], U8)
+        wp_grouped = sbuf("wp_grouped", [P, M, PACK], BF16)
+        for h in range(2):
+            interleave(wp_raw[h], False, wp_grouped[:, halves[h], :])
+        for q in range(T // P):
+            round_sums(q, 0)
+
+        out_view = out.rearrange("(f p) t -> p f t", p=P)
+
+        def project(t0, width, last):
+            c_grouped = sbuf("c_grouped%d" % t0, [P, width, PACK], BF16)
+            c_pairs = c_grouped[:].rearrange("p t j -> p (t j)").bitcast(F32)
+            for s in range(width // P):
+                q = t0 // P + s
+                round_sums(q, 1)
+                pairs = c_rows[q][:].rearrange("t u p e -> t (u p e)").bitcast(F32)
+                back = work_psum.tile([P, 2, P], F32, name="acc")
+                for u in range(2):
+                    nc.tensor.transpose(back[:, u, :], pairs[:, u * P:(u + 1) * P], identity[:])
+                nc.scalar.copy(out=c_pairs[:, 2 * s * P:2 * (s + 1) * P].rearrange("p (t u) -> p t u", u=2),
+                               in_=back[:].rearrange("p u t -> p t u"))
+            c_words = sbuf("c_words%d" % t0, [P, width], U32)
+            c_scales = sbuf("c_scales%d" % t0, [P, width], U8)
+            quantize(c_grouped, c_words[:], c_scales[:])
+            for g in range(2):
+                acc = work_psum.tile([P, 2, width], F32, name="acc")
+                for s in range(2):
+                    cols = slice((2 * g + s) * P, (2 * g + s + 1) * P)
+                    nc.tensor.matmul_mx(out=acc[:, s, :],
+                                        lhsT=wp_words[:, cols].bitcast(FP8X4), lhsT_scale=wp_scales[:, cols],
+                                        rhs=c_words[:].bitcast(FP8X4), rhs_scale=c_scales[:],
+                                        start=True, stop=True)
+                result = sbuf("result%d_%d" % (t0, g), [P, 2, width], F32)
+                if last and g == 1:
+                    nc.vector.tensor_copy(out=result[:], in_=acc[:])
+                else:
+                    nc.scalar.copy(out=result[:], in_=acc[:])
+                nc.sync.dma_start(out=out_view[:, 2 * g:2 * g + 2, t0:t0 + width], in_=result[:])
+
+        for n, (t0, width) in enumerate(TOKEN_GROUPS):
+            combine(2, t0, width)
+            combine(3, t0, width)
+            if n == 0:
+                quantize(wp_grouped, wp_words[:], wp_scales[:])
+            else:
+                project(TOKEN_GROUPS[n - 1][0], TOKEN_GROUPS[n - 1][1], False)
+        project(TOKEN_GROUPS[-1][0], TOKEN_GROUPS[-1][1], True)

@@ -34,8 +34,8 @@ PLACES = {
     "w_raw13": 32 * KIB, "w_grouped12": 32 * KIB, "products1_0": 32 * KIB,
     "y2": 38 * KIB + 64, "w_raw15": 44 * KIB, "y3": 48 * KIB - 64,
     "bias1": 54 * KIB, "wp_grouped": 54 * KIB,
-    "c_rows0": 58 * KIB, "products2_384": 58 * KIB,
-    "c_rows1": 60 * KIB, "products3_384": 60 * KIB,
+    "c_grouped0": 58 * KIB, "products3_384": 58 * KIB,
+    "c_rows1": 60 * KIB, "products2_384": 60 * KIB,
 }
 VECTOR_COPIES = ((1, 0), (1, 1))
 
@@ -65,8 +65,8 @@ def tile_moe_nxt_lin_relu_kernel(tc, xT, w, b, wp, gate, offs, pos1, pos2, pos3,
             return tile
 
         def interleave(raw, on_vector, grouped):
-            dst = grouped.rearrange("p (c i) j -> p c j i", i=2)
-            src = raw[:].rearrange("p j (c i) -> p c j i", i=2)
+            dst = grouped.rearrange("p (c i) j -> p c j i", i=4)
+            src = raw[:].rearrange("p j (c i) -> p c j i", i=4)
             if on_vector:
                 nc.vector.tensor_copy(out=dst, in_=src)
             else:
@@ -161,8 +161,14 @@ def tile_moe_nxt_lin_relu_kernel(tc, xT, w, b, wp, gate, offs, pos1, pos2, pos3,
                     nc.tensor.matmul(c_sum[t0 // P + s][:, r * P:(r + 1) * P], lhsT=product[:, s * P:(s + 1) * P],
                                      rhs=identity[:], is_transpose=True, start=(i == 0), stop=(i == TOP - 1))
 
-        def round_sums(q, h):
-            nc.scalar.copy(out=c_rows[q][:, :, h * 64:(h + 1) * 64, :],
+        def move(on_vector, out, in_):
+            if on_vector:
+                nc.vector.tensor_copy(out=out, in_=in_)
+            else:
+                nc.scalar.copy(out=out, in_=in_)
+
+        def round_sums(q, h, on_vector=False):
+            move(on_vector, out=c_rows[q][:, :, h * 64:(h + 1) * 64, :],
                            in_=c_sum[q][:, halves[h]].rearrange("t (p u e) -> t u p e", u=2, e=2))
 
         gather_tokens(0)
@@ -197,12 +203,12 @@ def tile_moe_nxt_lin_relu_kernel(tc, xT, w, b, wp, gate, offs, pos1, pos2, pos3,
             c_pairs = c_grouped[:].rearrange("p t j -> p (t j)").bitcast(F32)
             for s in range(width // P):
                 q = t0 // P + s
-                round_sums(q, 1)
+                round_sums(q, 1, last)
                 pairs = c_rows[q][:].rearrange("t u p e -> t (u p e)").bitcast(F32)
                 back = work_psum.tile([P, 2, P], F32, name="acc")
                 for u in range(2):
                     nc.tensor.transpose(back[:, u, :], pairs[:, u * P:(u + 1) * P], identity[:])
-                nc.scalar.copy(out=c_pairs[:, 2 * s * P:2 * (s + 1) * P].rearrange("p (t u) -> p t u", u=2),
+                move(last, out=c_pairs[:, 2 * s * P:2 * (s + 1) * P].rearrange("p (t u) -> p t u", u=2),
                                in_=back[:].rearrange("p u t -> p t u"))
             c_words = sbuf("c_words%d" % t0, [P, width], U32)
             c_scales = sbuf("c_scales%d" % t0, [P, width], U8)
@@ -216,17 +222,16 @@ def tile_moe_nxt_lin_relu_kernel(tc, xT, w, b, wp, gate, offs, pos1, pos2, pos3,
                                         rhs=c_words[:].bitcast(FP8X4), rhs_scale=c_scales[:],
                                         start=True, stop=True)
                 result = sbuf("result%d_%d" % (t0, g), [P, 2, width], F32)
-                if last and g == 1:
-                    nc.vector.tensor_copy(out=result[:], in_=acc[:])
-                else:
-                    nc.scalar.copy(out=result[:], in_=acc[:])
+                move(last and g == 1, out=result[:], in_=acc[:])
                 nc.sync.dma_start(out=out_view[:, 2 * g:2 * g + 2, t0:t0 + width], in_=result[:])
 
-        for n, (t0, width) in enumerate(TOKEN_GROUPS):
-            combine(2, t0, width)
-            combine(3, t0, width)
-            if n == 0:
-                quantize(wp_grouped, wp_words[:], wp_scales[:])
-            else:
-                project(TOKEN_GROUPS[n - 1][0], TOKEN_GROUPS[n - 1][1], False)
-        project(TOKEN_GROUPS[-1][0], TOKEN_GROUPS[-1][1], True)
+        combine(2, 0, 256)
+        combine(3, 0, 256)
+        quantize(wp_grouped, wp_words[:], wp_scales[:])
+        combine(2, 256, 128)
+        combine(3, 256, 128)
+        project(0, 256, False)
+        combine(2, 384, 128)
+        combine(3, 384, 128)
+        project(256, 128, False)
+        project(384, 128, True)

@@ -23,21 +23,23 @@ P = 128
 PACK = 4
 HALF = 256
 LIST_ROWS = 16
-TOKEN_GROUPS = ((0, 256), (256, 128), (384, 128))
+WALK = 4
+BANK = 2048
+WORK_BANKS = 4
+WHOLE_LOADS = 4
+X_SPLIT = 336
 KIB = 1024
 PLACES = {
-    "w_grouped00": 0, "slot_words1": 0, "slot_scales1": 2 * KIB,
-    "w_grouped01": 4 * KIB, "slot_words2": 4 * KIB, "slot_scales2": 6 * KIB,
-    "w_grouped02": 8 * KIB, "w_grouped10": 8 * KIB,
-    "y0": 12 * KIB + 64, "w_raw03": 18 * KIB, "y1": 22 * KIB - 64,
-    "bias0": 28 * KIB, "w_grouped11": 28 * KIB,
-    "w_raw13": 32 * KIB, "w_grouped12": 32 * KIB, "products1_0": 32 * KIB,
-    "y2": 38 * KIB + 64, "w_raw15": 44 * KIB, "y3": 48 * KIB - 64,
-    "bias1": 54 * KIB, "wp_grouped": 54 * KIB,
-    "c_grouped0": 58 * KIB, "products3_384": 58 * KIB,
-    "c_rows1": 60 * KIB, "products2_384": 60 * KIB,
+    "x_grouped": 3 * KIB, "w_grouped0_0": 0, "w_grouped0_2": 4 * KIB, "w_grouped1_0": 6 * KIB,
+    "slot_words2": 0, "slot_scales2": 2 * KIB,
+    "w_words0_0": 16 * KIB - 64, "w_grouped0_3": 14 * KIB, "w_grouped0_4": 16 * KIB, "w_grouped1_2": 12 * KIB,
+    "w_scales0_0": 18 * KIB, "w_grouped0_5": 18 * KIB,
+    "bias0": 20 * KIB, "w_grouped1_4": 20 * KIB, "products1_0": 20 * KIB,
+    "y2": 26 * KIB + 64, "w_raw1_5": 32 * KIB, "y3": 36 * KIB - 64,
+    "bias1": 42 * KIB, "wp_grouped": 42 * KIB,
+    "c_grouped0": 46 * KIB, "products3_384": 46 * KIB,
+    "c_rows1": 48 * KIB, "products2_384": 48 * KIB,
 }
-VECTOR_COPIES = ((1, 0), (1, 1))
 
 
 def tile_moe_nxt_lin_relu_kernel(tc, xT, w, b, wp, gate, offs, pos1, pos2, pos3, out):
@@ -46,7 +48,7 @@ def tile_moe_nxt_lin_relu_kernel(tc, xT, w, b, wp, gate, offs, pos1, pos2, pos3,
         lists = ctx.enter_context(tc.tile_pool(name="lists", bufs=1))
         keep = ctx.enter_context(tc.tile_pool(name="keep", bufs=1))
         shared = ctx.enter_context(tc.tile_pool(name="shared", bufs=1))
-        work_psum = ctx.enter_context(tc.psum_pool(name="work_psum", bufs=4))
+        work_psum = ctx.enter_context(tc.psum_pool(name="work_psum", bufs=1))
         sum_psum = ctx.enter_context(tc.psum_pool(name="sum_psum", bufs=1))
 
         def sbuf(name, shape, dtype):
@@ -54,8 +56,15 @@ def tile_moe_nxt_lin_relu_kernel(tc, xT, w, b, wp, gate, offs, pos1, pos2, pos3,
                 return shared.tile(shape, dtype, name=name, align_bytes=64, offset=PLACES[name])
             return keep.tile(shape, dtype, name=name, align_bytes=64)
 
+        work_tiles = []
+
+        def work_bank(width):
+            turn = len(work_tiles)
+            work_tiles.append(work_psum.tile([P, 2, width], F32, name="work%d" % turn, offset=(turn % WORK_BANKS) * BANK))
+            return work_tiles[turn]
+
         def load_rows(name, rows):
-            raw = sbuf(name, [P, PACK, HALF], F32)
+            raw = sbuf(name, [P, PACK, rows.shape[1]], F32)
             nc.sync.dma_start(out=raw[:], in_=rows.rearrange("(p j) c -> p j c", j=PACK))
             return raw
 
@@ -65,37 +74,47 @@ def tile_moe_nxt_lin_relu_kernel(tc, xT, w, b, wp, gate, offs, pos1, pos2, pos3,
             return tile
 
         def interleave(raw, on_vector, grouped):
-            dst = grouped.rearrange("p (c i) j -> p c j i", i=4)
-            src = raw[:].rearrange("p j (c i) -> p c j i", i=4)
+            dst = grouped.rearrange("p (c i) j -> p c j i", i=WALK)
+            src = raw.rearrange("p j (c i) -> p c j i", i=WALK)
             if on_vector:
                 nc.vector.tensor_copy(out=dst, in_=src)
             else:
                 nc.scalar.activation(out=dst, in_=src, func=COPY)
 
-        def quantize(grouped, codes, scales):
-            nc.vector.quantize_mx(out=codes.bitcast(FP8X4), scales=scales,
+        def quantize(grouped, words, scales):
+            nc.vector.quantize_mx(out=words.bitcast(FP8X4), scales=scales,
                                   in_=grouped[:].rearrange("p c j -> p (c j)"))
 
-        halves = [slice(h * HALF, (h + 1) * HALF) for h in range(2)]
+        def move(on_vector, dst, src):
+            if on_vector:
+                nc.vector.tensor_copy(out=dst, in_=src)
+            else:
+                nc.scalar.copy(out=dst, in_=src)
 
-        x_raw = [load_rows("x_raw%d" % h, xT[:, halves[h]]) for h in range(2)]
+        halves = [slice(h * HALF, (h + 1) * HALF) for h in range(2)]
+        bias = [sbuf("bias%d" % h, [P, 2, E], F32) for h in range(2)]
+
+        def load_bias(h):
+            nc.sync.dma_start(out=bias[h][:], in_=b[halves[h], :].rearrange("(s p) e -> p s e", p=P))
+
+        x_raw = load_rows("x_raw", xT)
         slot_tokens = load_list("slot_tokens", offs)
         w_raw = {}
-        w_raw[0, 0] = load_rows("w_raw00", w[0][:, halves[0]])
-        w_raw[0, 1] = load_rows("w_raw01", w[1][:, halves[0]])
-        bias = [sbuf("bias%d" % h, [P, 2, E], F32) for h in range(2)]
-        for h in range(2):
-            nc.sync.dma_start(out=bias[h][:], in_=b[halves[h], :].rearrange("(s p) e -> p s e", p=P))
-        for e in range(2, E):
-            w_raw[0, e] = load_rows("w_raw0%d" % e, w[e][:, halves[0]])
-        for e in range(2):
-            w_raw[1, e] = load_rows("w_raw1%d" % e, w[e][:, halves[1]])
+        for e in range(WHOLE_LOADS):
+            whole = load_rows("w_raw%d" % e, w[e])
+            for h in range(2):
+                w_raw[h, e] = whole[:, :, halves[h]]
+            if e == 0:
+                load_bias(0)
+        for e in range(WHOLE_LOADS, E):
+            w_raw[0, e] = load_rows("w_raw0_%d" % e, w[e][:, halves[0]])[:]
         token_slots = [load_list("token_slots%d" % i, src) for i, src in enumerate((pos1, pos2, pos3))]
         gates = sbuf("gates", [P, TOP, T], F32)
         nc.sync.dma_start(out=gates[:], in_=gate[:, 0:P, :].rearrange("i p t -> p i t"))
-        for e in range(2, E):
-            w_raw[1, e] = load_rows("w_raw1%d" % e, w[e][:, halves[1]])
-        wp_raw = [load_rows("wp_raw%d" % h, wp[:, halves[h]]) for h in range(2)]
+        load_bias(1)
+        for e in range(WHOLE_LOADS, E):
+            w_raw[1, e] = load_rows("w_raw1_%d" % e, w[e][:, halves[1]])[:]
+        wp_raw = load_rows("wp_raw", wp)
 
         identity = sbuf("identity", [P, P], F32)
         make_identity(nc, identity[:])
@@ -104,14 +123,14 @@ def tile_moe_nxt_lin_relu_kernel(tc, xT, w, b, wp, gate, offs, pos1, pos2, pos3,
         x_scales = sbuf("x_scales", [P, 2 * T], U8)
         nc.gpsimd.memset(x_words[:, T:], 0)
         nc.gpsimd.memset(x_scales[:].bitcast(I32), 0)
-        for h in range(2):
-            x_grouped = sbuf("x_grouped%d" % h, [P, HALF, PACK], BF16)
-            interleave(x_raw[h], True, x_grouped[:])
-            quantize(x_grouped, x_words[:, halves[h]], x_scales[:, halves[h]])
+        x_grouped = sbuf("x_grouped", [P, T, PACK], BF16)
+        interleave(x_raw[:, :, :X_SPLIT], True, x_grouped[:, :X_SPLIT, :])
+        interleave(x_raw[:, :, X_SPLIT:], False, x_grouped[:, X_SPLIT:, :])
+        quantize(x_grouped, x_words[:, :T], x_scales[:, :T])
 
         y = [sbuf("y%d" % r, [P, S], F32) for r in range(N // P)]
         slot_words, slot_scales = {}, {}
-        w_words, w_scales = {}, {}
+        w_grouped, w_words, w_scales = {}, {}, {}
 
         def gather_tokens(pair):
             cols = slice(pair * 2 * C // LIST_ROWS, (pair + 1) * 2 * C // LIST_ROWS)
@@ -120,22 +139,26 @@ def tile_moe_nxt_lin_relu_kernel(tc, xT, w, b, wp, gate, offs, pos1, pos2, pos3,
             nc.vector.tensor_copy(slot_words[pair][:], x_words[:].indirect(slot_tokens[:, cols]))
             nc.vector.tensor_copy(slot_scales[pair][:], x_scales[:].indirect(slot_tokens[:, cols]))
 
-        def quantize_weights(h, pair):
-            grouped = sbuf("w_grouped%d%d" % (h, pair), [P, 2 * HALF, PACK], BF16)
-            for n in range(2):
-                e = 2 * pair + n
-                interleave(w_raw[h, e], (h, e) in VECTOR_COPIES, grouped[:, halves[n], :])
-            w_words[h, pair] = sbuf("w_words%d%d" % (h, pair), [P, 2 * HALF], U32)
-            w_scales[h, pair] = sbuf("w_scales%d%d" % (h, pair), [P, 2 * HALF], U8)
-            quantize(grouped, w_words[h, pair][:], w_scales[h, pair][:])
+        def round_weights(h, e, first, count, on_vector=False):
+            if e == first:
+                w_grouped[h, first] = sbuf("w_grouped%d_%d" % (h, first), [P, count * HALF, PACK], BF16)
+            interleave(w_raw[h, e], on_vector, w_grouped[h, first][:, halves[e - first], :])
+
+        def quantize_weights(h, first, count):
+            words = sbuf("w_words%d_%d" % (h, first), [P, count * HALF], U32)
+            scales = sbuf("w_scales%d_%d" % (h, first), [P, count * HALF], U8)
+            quantize(w_grouped[h, first], words[:], scales[:])
+            for n in range(count):
+                w_words[h, first + n] = words[:, halves[n]]
+                w_scales[h, first + n] = scales[:, halves[n]]
 
         def expert(h, e):
-            acc = work_psum.tile([P, 2, C], F32, name="acc")
+            acc = work_bank(C)
             mine = slice((e % 2) * C, (e % 2 + 1) * C)
             for s in range(2):
-                cols = slice((e % 2) * HALF + s * P, (e % 2) * HALF + (s + 1) * P)
+                cols = slice(s * P, (s + 1) * P)
                 nc.tensor.matmul_mx(out=acc[:, s, :],
-                                    lhsT=w_words[h, e // 2][:, cols].bitcast(FP8X4), lhsT_scale=w_scales[h, e // 2][:, cols],
+                                    lhsT=w_words[h, e][:, cols].bitcast(FP8X4), lhsT_scale=w_scales[h, e][:, cols],
                                     rhs=slot_words[e // 2][:, mine].bitcast(FP8X4), rhs_scale=slot_scales[e // 2][:, mine],
                                     start=True, stop=True)
             return acc
@@ -143,9 +166,8 @@ def tile_moe_nxt_lin_relu_kernel(tc, xT, w, b, wp, gate, offs, pos1, pos2, pos3,
         def expert_pair(h, pair):
             accs = [(e, expert(h, e)) for e in (2 * pair, 2 * pair + 1)]
             for s in range(2):
-                r = 2 * h + s
                 for e, acc in accs:
-                    nc.scalar.activation(out=y[r][:, e * C:(e + 1) * C], in_=acc[:, s, :], func=RELU,
+                    nc.scalar.activation(out=y[2 * h + s][:, e * C:(e + 1) * C], in_=acc[:, s, :], func=RELU,
                                          bias=bias[h][:, s, e:e + 1])
 
         c_sum = [sum_psum.tile([P, N], F32, name="c_sum%d" % q) for q in range(T // P)]
@@ -161,29 +183,37 @@ def tile_moe_nxt_lin_relu_kernel(tc, xT, w, b, wp, gate, offs, pos1, pos2, pos3,
                     nc.tensor.matmul(c_sum[t0 // P + s][:, r * P:(r + 1) * P], lhsT=product[:, s * P:(s + 1) * P],
                                      rhs=identity[:], is_transpose=True, start=(i == 0), stop=(i == TOP - 1))
 
-        def move(on_vector, out, in_):
-            if on_vector:
-                nc.vector.tensor_copy(out=out, in_=in_)
-            else:
-                nc.scalar.copy(out=out, in_=in_)
-
-        def round_sums(q, h, on_vector=False):
-            move(on_vector, out=c_rows[q][:, :, h * 64:(h + 1) * 64, :],
-                           in_=c_sum[q][:, halves[h]].rearrange("t (p u e) -> t u p e", u=2, e=2))
+        def round_sums(q, h, on_vector):
+            move(on_vector, c_rows[q][:, :, h * 64:(h + 1) * 64, :],
+                 c_sum[q][:, halves[h]].rearrange("t (p u e) -> t u p e", u=2, e=2))
 
         gather_tokens(0)
-        for pair in range(E // 2):
-            quantize_weights(0, pair)
-            if pair + 1 < E // 2:
-                gather_tokens(pair + 1)
-            if pair > 0:
-                expert_pair(0, pair - 1)
-        expert_pair(0, E // 2 - 1)
+        gather_tokens(1)
+        for e in range(2):
+            for h in range(2):
+                round_weights(h, e, 0, 2)
+        quantize_weights(0, 0, 2)
+        gather_tokens(2)
+        quantize_weights(1, 0, 2)
+        round_weights(0, 2, 2, 1)
+        quantize_weights(0, 2, 1)
+        expert_pair(0, 0)
+        round_weights(0, 3, 3, 1)
+        quantize_weights(0, 3, 1)
+        round_weights(1, 2, 2, 2, True)
+        round_weights(0, 4, 4, 1)
+        quantize_weights(0, 4, 1)
+        round_weights(1, 3, 2, 2, True)
+        round_weights(0, 5, 5, 1)
+        quantize_weights(0, 5, 1)
+        expert_pair(0, 1)
+        expert_pair(0, 2)
+        quantize_weights(1, 2, 2)
 
-        quantize_weights(1, 0)
         combine(0, 0, T)
-        quantize_weights(1, 1)
-        quantize_weights(1, 2)
+        for e in range(4, E):
+            round_weights(1, e, 4, 2)
+        quantize_weights(1, 4, 2)
         for pair in range(E // 2):
             expert_pair(1, pair)
         combine(1, 0, T)
@@ -192,9 +222,9 @@ def tile_moe_nxt_lin_relu_kernel(tc, xT, w, b, wp, gate, offs, pos1, pos2, pos3,
         wp_scales = sbuf("wp_scales", [P, M], U8)
         wp_grouped = sbuf("wp_grouped", [P, M, PACK], BF16)
         for h in range(2):
-            interleave(wp_raw[h], False, wp_grouped[:, halves[h], :])
+            interleave(wp_raw[:, :, halves[h]], False, wp_grouped[:, halves[h], :])
         for q in range(T // P):
-            round_sums(q, 0)
+            round_sums(q, 0, False)
 
         out_view = out.rearrange("(f p) t -> p f t", p=P)
 
@@ -205,16 +235,16 @@ def tile_moe_nxt_lin_relu_kernel(tc, xT, w, b, wp, gate, offs, pos1, pos2, pos3,
                 q = t0 // P + s
                 round_sums(q, 1, last)
                 pairs = c_rows[q][:].rearrange("t u p e -> t (u p e)").bitcast(F32)
-                back = work_psum.tile([P, 2, P], F32, name="acc")
+                back = work_bank(P)
                 for u in range(2):
                     nc.tensor.transpose(back[:, u, :], pairs[:, u * P:(u + 1) * P], identity[:])
-                move(last, out=c_pairs[:, 2 * s * P:2 * (s + 1) * P].rearrange("p (t u) -> p t u", u=2),
-                               in_=back[:].rearrange("p u t -> p t u"))
+                move(last, c_pairs[:, 2 * s * P:2 * (s + 1) * P].rearrange("p (t u) -> p t u", u=2),
+                     back[:].rearrange("p u t -> p t u"))
             c_words = sbuf("c_words%d" % t0, [P, width], U32)
             c_scales = sbuf("c_scales%d" % t0, [P, width], U8)
             quantize(c_grouped, c_words[:], c_scales[:])
             for g in range(2):
-                acc = work_psum.tile([P, 2, width], F32, name="acc")
+                acc = work_bank(width)
                 for s in range(2):
                     cols = slice((2 * g + s) * P, (2 * g + s + 1) * P)
                     nc.tensor.matmul_mx(out=acc[:, s, :],
@@ -222,7 +252,7 @@ def tile_moe_nxt_lin_relu_kernel(tc, xT, w, b, wp, gate, offs, pos1, pos2, pos3,
                                         rhs=c_words[:].bitcast(FP8X4), rhs_scale=c_scales[:],
                                         start=True, stop=True)
                 result = sbuf("result%d_%d" % (t0, g), [P, 2, width], F32)
-                move(last and g == 1, out=result[:], in_=acc[:])
+                move(last and g == 1, result[:], acc[:])
                 nc.sync.dma_start(out=out_view[:, 2 * g:2 * g + 2, t0:t0 + width], in_=result[:])
 
         combine(2, 0, 256)

from contextlib import ExitStack

import concourse.mybir as mybir
from concourse.masks import make_identity

K, T, E, C, N, M = 512, 512, 6, 256, 512, 512
TOP = 3
S = E * C
FLOPS = 2 * K * N * S + 2 * N * M * T

F32 = mybir.dt.float32
BF16 = mybir.dt.bfloat16
I32 = mybir.dt.int32
U32 = mybir.dt.uint32
U16 = mybir.dt.uint16
U8 = mybir.dt.uint8
FP8X4 = mybir.dt.float8_e4m3fn_x4
RELU = mybir.ActivationFunctionType.Relu
COPY = mybir.ActivationFunctionType.Copy
MULT = mybir.AluOpType.mult

P = 128
PACK = 4
HALF = 256
LIST_ROWS = 16
WALK = 4
BANK = 2048
WORK_BANKS = 4
WHOLE_LOADS = 4
X_SPLIT = 336
KIB = 1024
PLACES = {
    "x_grouped": 3 * KIB, "w_grouped0_0": 0, "w_grouped0_2": 4 * KIB, "w_grouped1_0": 6 * KIB,
    "slot_words2": 0, "slot_scales2": 2 * KIB,
    "w_words0_0": 16 * KIB - 64, "w_grouped0_3": 14 * KIB, "w_grouped0_4": 16 * KIB, "w_grouped1_2": 12 * KIB,
    "w_scales0_0": 18 * KIB, "w_grouped0_5": 18 * KIB,
    "bias0": 20 * KIB, "w_grouped1_4": 20 * KIB, "products1_0": 20 * KIB,
    "y2": 26 * KIB + 64, "w_raw1_5": 32 * KIB, "y3": 36 * KIB - 64,
    "bias1": 42 * KIB, "wp_grouped": 42 * KIB,
    "c_grouped0": 46 * KIB, "products3_384": 46 * KIB,
    "c_rows1": 48 * KIB, "products2_384": 48 * KIB,
}


def tile_moe_nxt_lin_relu_kernel(tc, xT, w, b, wp, gate, offs, pos1, pos2, pos3, out):
    nc = tc.nc
    with ExitStack() as ctx:
        lists = ctx.enter_context(tc.tile_pool(name="lists", bufs=1))
        keep = ctx.enter_context(tc.tile_pool(name="keep", bufs=1))
        shared = ctx.enter_context(tc.tile_pool(name="shared", bufs=1))
        work_psum = ctx.enter_context(tc.psum_pool(name="work_psum", bufs=1))
        sum_psum = ctx.enter_context(tc.psum_pool(name="sum_psum", bufs=1))

        def sbuf(name, shape, dtype):
            if name in PLACES:
                return shared.tile(shape, dtype, name=name, align_bytes=64, offset=PLACES[name])
            return keep.tile(shape, dtype, name=name, align_bytes=64)

        work_tiles = []

        def work_bank(width):
            turn = len(work_tiles)
            work_tiles.append(work_psum.tile([P, 2, width], F32, name="work%d" % turn, offset=(turn % WORK_BANKS) * BANK))
            return work_tiles[turn]

        def load_rows(name, rows):
            raw = sbuf(name, [P, PACK, rows.shape[1]], F32)
            nc.sync.dma_start(out=raw[:], in_=rows.rearrange("(p j) c -> p j c", j=PACK))
            return raw

        def load_list(name, src):
            tile = lists.tile(list(src.shape), U16, name=name)
            nc.sync.dma_start(tile[:], src)
            return tile

        def interleave(raw, on_vector, grouped):
            dst = grouped.rearrange("p (c i) j -> p c j i", i=WALK)
            src = raw.rearrange("p j (c i) -> p c j i", i=WALK)
            if on_vector:
                nc.vector.tensor_copy(out=dst, in_=src)
            else:
                nc.scalar.activation(out=dst, in_=src, func=COPY)

        def quantize(grouped, words, scales):
            nc.vector.quantize_mx(out=words.bitcast(FP8X4), scales=scales,
                                  in_=grouped[:].rearrange("p c j -> p (c j)"))

        def move(on_vector, dst, src):
            if on_vector:
                nc.vector.tensor_copy(out=dst, in_=src)
            else:
                nc.scalar.copy(out=dst, in_=src)

        halves = [slice(h * HALF, (h + 1) * HALF) for h in range(2)]
        bias = [sbuf("bias%d" % h, [P, 2, E], F32) for h in range(2)]

        def load_bias(h):
            nc.sync.dma_start(out=bias[h][:], in_=b[halves[h], :].rearrange("(s p) e -> p s e", p=P))

        x_raw = load_rows("x_raw", xT)
        slot_tokens = load_list("slot_tokens", offs)
        w_raw = {}
        for e in range(WHOLE_LOADS):
            whole = load_rows("w_raw%d" % e, w[e])
            for h in range(2):
                w_raw[h, e] = whole[:, :, halves[h]]
            if e == 0:
                load_bias(0)
        for e in range(WHOLE_LOADS, E):
            w_raw[0, e] = load_rows("w_raw0_%d" % e, w[e][:, halves[0]])[:]
        token_slots = [load_list("token_slots%d" % i, src) for i, src in enumerate((pos1, pos2, pos3))]
        gates = sbuf("gates", [P, TOP, T], F32)
        nc.sync.dma_start(out=gates[:], in_=gate[:, 0:P, :].rearrange("i p t -> p i t"))
        load_bias(1)
        for e in range(WHOLE_LOADS, E):
            w_raw[1, e] = load_rows("w_raw1_%d" % e, w[e][:, halves[1]])[:]
        wp_raw = load_rows("wp_raw", wp)

        identity = sbuf("identity", [P, P], F32)
        make_identity(nc, identity[:])

        x_words = sbuf("x_words", [P, 2 * T], U32)
        x_scales = sbuf("x_scales", [P, 2 * T], U8)
        nc.gpsimd.memset(x_words[:, T:], 0)
        nc.gpsimd.memset(x_scales[:].bitcast(I32), 0)
        x_grouped = sbuf("x_grouped", [P, T, PACK], BF16)
        interleave(x_raw[:, :, :X_SPLIT], True, x_grouped[:, :X_SPLIT, :])
        interleave(x_raw[:, :, X_SPLIT:], False, x_grouped[:, X_SPLIT:, :])
        quantize(x_grouped, x_words[:, :T], x_scales[:, :T])

        y = [sbuf("y%d" % r, [P, S], F32) for r in range(N // P)]
        slot_words, slot_scales = {}, {}
        w_grouped, w_words, w_scales = {}, {}, {}

        def gather_tokens(pair):
            cols = slice(pair * 2 * C // LIST_ROWS, (pair + 1) * 2 * C // LIST_ROWS)
            slot_words[pair] = sbuf("slot_words%d" % pair, [P, 2 * C], U32)
            slot_scales[pair] = sbuf("slot_scales%d" % pair, [P, 2 * C], U8)
            nc.vector.tensor_copy(slot_words[pair][:], x_words[:].indirect(slot_tokens[:, cols]))
            nc.vector.tensor_copy(slot_scales[pair][:], x_scales[:].indirect(slot_tokens[:, cols]))

        def round_weights(h, e, first, count, on_vector=False):
            if e == first:
                w_grouped[h, first] = sbuf("w_grouped%d_%d" % (h, first), [P, count * HALF, PACK], BF16)
            interleave(w_raw[h, e], on_vector, w_grouped[h, first][:, halves[e - first], :])

        def quantize_weights(h, first, count):
            words = sbuf("w_words%d_%d" % (h, first), [P, count * HALF], U32)
            scales = sbuf("w_scales%d_%d" % (h, first), [P, count * HALF], U8)
            quantize(w_grouped[h, first], words[:], scales[:])
            for n in range(count):
                w_words[h, first + n] = words[:, halves[n]]
                w_scales[h, first + n] = scales[:, halves[n]]

        def expert(h, e):
            acc = work_bank(C)
            mine = slice((e % 2) * C, (e % 2 + 1) * C)
            for s in range(2):
                cols = slice(s * P, (s + 1) * P)
                nc.tensor.matmul_mx(out=acc[:, s, :],
                                    lhsT=w_words[h, e][:, cols].bitcast(FP8X4), lhsT_scale=w_scales[h, e][:, cols],
                                    rhs=slot_words[e // 2][:, mine].bitcast(FP8X4), rhs_scale=slot_scales[e // 2][:, mine],
                                    start=True, stop=True)
            return acc

        def expert_pair(h, pair):
            accs = [(e, expert(h, e)) for e in (2 * pair, 2 * pair + 1)]
            for s in range(2):
                for e, acc in accs:
                    nc.scalar.activation(out=y[2 * h + s][:, e * C:(e + 1) * C], in_=acc[:, s, :], func=RELU,
                                         bias=bias[h][:, s, e:e + 1])

        c_sum = [sum_psum.tile([P, N], F32, name="c_sum%d" % q) for q in range(T // P)]
        c_rows = [sbuf("c_rows%d" % q, [P, 2, P, 2], BF16) for q in range(T // P)]

        def combine(r, t0, width):
            products = sbuf("products%d_%d" % (r, t0), [P, TOP, width], F32)
            for i in range(TOP):
                product = products[:, i, :]
                offsets = token_slots[i][:, t0 // LIST_ROWS:(t0 + width) // LIST_ROWS]
                nc.vector.tensor_tensor(product, y[r][:].indirect(offsets), gates[:, i, t0:t0 + width], MULT)
                for s in range(width // P):
                    nc.tensor.matmul(c_sum[t0 // P + s][:, r * P:(r + 1) * P], lhsT=product[:, s * P:(s + 1) * P],
                                     rhs=identity[:], is_transpose=True, start=(i == 0), stop=(i == TOP - 1))

        def round_sums(q, h, on_vector):
            move(on_vector, c_rows[q][:, :, h * 64:(h + 1) * 64, :],
                 c_sum[q][:, halves[h]].rearrange("t (p u e) -> t u p e", u=2, e=2))

        gather_tokens(0)
        gather_tokens(1)
        for e in range(2):
            for h in range(2):
                round_weights(h, e, 0, 2)
        quantize_weights(0, 0, 2)
        gather_tokens(2)
        quantize_weights(1, 0, 2)
        round_weights(0, 2, 2, 1)
        quantize_weights(0, 2, 1)
        expert_pair(0, 0)
        round_weights(0, 3, 3, 1)
        quantize_weights(0, 3, 1)
        round_weights(1, 2, 2, 2, True)
        round_weights(0, 4, 4, 1)
        quantize_weights(0, 4, 1)
        round_weights(1, 3, 2, 2, True)
        round_weights(0, 5, 5, 1)
        quantize_weights(0, 5, 1)
        expert_pair(0, 1)
        expert_pair(0, 2)
        quantize_weights(1, 2, 2)

        combine(0, 0, T)
        for e in range(4, E):
            round_weights(1, e, 4, 2)
        quantize_weights(1, 4, 2)
        for pair in range(E // 2):
            expert_pair(1, pair)
        combine(1, 0, T)

        wp_words = sbuf("wp_words", [P, M], U32)
        wp_scales = sbuf("wp_scales", [P, M], U8)
        wp_grouped = sbuf("wp_grouped", [P, M, PACK], BF16)
        for h in range(2):
            interleave(wp_raw[:, :, halves[h]], False, wp_grouped[:, halves[h], :])
        for q in range(T // P):
            round_sums(q, 0, False)

        out_view = out.rearrange("(f p) t -> p f t", p=P)

        def project(t0, width, last):
            c_grouped = sbuf("c_grouped%d" % t0, [P, width, PACK], BF16)
            c_pairs = c_grouped[:].rearrange("p t j -> p (t j)").bitcast(F32)
            for s in range(width // P):
                q = t0 // P + s
                round_sums(q, 1, last)
                pairs = c_rows[q][:].rearrange("t u p e -> t (u p e)").bitcast(F32)
                back = work_bank(P)
                for u in range(2):
                    nc.tensor.transpose(back[:, u, :], pairs[:, u * P:(u + 1) * P], identity[:])
                move(last, c_pairs[:, 2 * s * P:2 * (s + 1) * P].rearrange("p (t u) -> p t u", u=2),
                     back[:].rearrange("p u t -> p t u"))
            c_words = sbuf("c_words%d" % t0, [P, width], U32)
            c_scales = sbuf("c_scales%d" % t0, [P, width], U8)
            quantize(c_grouped, c_words[:], c_scales[:])
            for g in range(2):
                acc = work_bank(width)
                for s in range(2):
                    cols = slice((2 * g + s) * P, (2 * g + s + 1) * P)
                    nc.tensor.matmul_mx(out=acc[:, s, :],
                                        lhsT=wp_words[:, cols].bitcast(FP8X4), lhsT_scale=wp_scales[:, cols],
                                        rhs=c_words[:].bitcast(FP8X4), rhs_scale=c_scales[:],
                                        start=True, stop=True)
                result = sbuf("result%d_%d" % (t0, g), [P, 2, width], F32)
                move(last and g == 1, result[:], acc[:])
                nc.sync.dma_start(out=out_view[:, 2 * g:2 * g + 2, t0:t0 + width], in_=result[:])

        combine(2, 0, 256)
        combine(3, 0, 256)
        quantize(wp_grouped, wp_words[:], wp_scales[:])
        combine(2, 256, 128)
        combine(3, 256, 128)
        project(0, 256, False)
        combine(2, 384, 128)
        combine(3, 384, 128)
        project(256, 128, False)
        project(384, 128, True)
